import numpy as np
import ml_dtypes


def mxq(x, axis, fmt="e4m3"):
    dtype, down = {"e4m3": (ml_dtypes.float8_e4m3fn, 7), "e5m2": (ml_dtypes.float8_e5m2, 14)}[fmt]
    v = np.moveaxis(np.asarray(x, np.float32).astype(ml_dtypes.bfloat16).astype(np.float64), axis, -1)
    blocks = v.reshape(v.shape[:-1] + (-1, 32))
    amax = np.abs(blocks).max(-1, keepdims=True)
    byte = np.maximum(np.where(amax > 0, np.frexp(amax)[1] - 1 + 127, 0) - down, 1)
    scale = np.exp2(byte - 127.0)
    codes = (blocks / scale).astype(np.float32).astype(dtype).astype(np.float64)
    return np.moveaxis((codes * scale).reshape(v.shape), -1, axis)


WIDE = False


def mx_kscale(k):
    if not WIDE:
        return np.ones(k)
    levels = np.array([30, -30])
    if k % 512:
        return np.exp2(np.random.permutation(np.resize(levels, k // 32))).repeat(32)
    a = np.empty((k // 512, 16))
    for p in range(k // 512):
        a[p, :8] = np.random.permutation(np.resize(levels, 8))
        for g in range(8):
            far = levels[np.abs(levels - a[p, g]) >= 10]
            a[p, g + 8] = far[np.random.randint(len(far))]
    return np.exp2(a.ravel()).repeat(32)


def f64(x):
    return np.asarray(x).astype(np.float64)


def striped(idx):
    return np.tile(np.asarray(idx).reshape(-1, 16).T, (8, 1)).astype(np.uint16)


def unstriped(offs):
    return offs[:16].T.reshape(-1).astype(np.int64)


E2M1 = np.array([0.0, 0.5, 1.0, 1.5, 2.0, 3.0, 4.0, 6.0, -0.0, -0.5, -1.0, -1.5, -2.0, -3.0, -4.0, -6.0])


def pack_weight(w, fmt):
    k, n = w.shape
    w = f64(np.asarray(w, np.float32).astype(ml_dtypes.bfloat16)).reshape(k // 32, 32, n)
    amax = np.abs(w).max(1)
    if fmt in ("e4m3", "e5m2"):
        byte = np.frexp(amax)[1] - 1 + 127 - (7 if fmt == "e4m3" else 14)
    else:
        mant, ex = np.frexp(amax / 6.0)
        byte = np.where(mant > 0.5, ex, ex - 1) + 127
    byte = np.clip(np.where(amax > 0, byte, 1), 1, 254)
    scaled = (w * np.exp2(127.0 - byte)[:, None, :]).reshape(k, n).astype(np.float32)
    by_word = np.ascontiguousarray(scaled.reshape(k // 512, 128, 4, n).transpose(0, 1, 3, 2))
    if fmt in ("e4m3", "e5m2"):
        words = by_word.astype(ml_dtypes.float8_e4m3fn if fmt == "e4m3" else ml_dtypes.float8_e5m2).view(np.uint8)
    else:
        c = by_word.astype(ml_dtypes.float4_e2m1fn).view(np.uint8) & 0xF
        words = (c[..., 0::2] | (c[..., 1::2] << 4)).reshape(k // 512, 128, 2 * n)
    return np.ascontiguousarray(words), np.ascontiguousarray(byte.astype(np.uint8).reshape(k // 512, 16, n))


def unpack_weight(words, scales, fmt):
    g, _, n = scales.shape
    words = np.ascontiguousarray(words).reshape(g, 128, n, -1)
    if fmt in ("e4m3", "e5m2"):
        vals = words.view(ml_dtypes.float8_e4m3fn if fmt == "e4m3" else ml_dtypes.float8_e5m2).astype(np.float64)
    else:
        nib = np.empty((g, 128, n, 4), np.uint8)
        nib[..., 0::2] = words & 0xF
        nib[..., 1::2] = words >> 4
        vals = E2M1[nib]
    vals = vals * np.repeat(np.exp2(scales.astype(np.float64) - 127.0), 8, axis=1)[..., None]
    return vals.transpose(0, 1, 3, 2).reshape(g * 512, n)


K, T, Z, J, R, C, O, N, L, E = 512, 1024, 1024, 256, 512, 512, 256, 256, 512, 128


def setup_inputs():
    n = np.random.standard_normal
    idx = np.random.permutation(T)[:J]
    idx2 = np.random.permutation(Z)[:J]
    idx3 = np.random.permutation(C)[:J]
    idx4 = np.random.permutation(C)[:J]
    idx5 = np.random.permutation(C)[:O]
    idx6 = np.random.permutation(O)[:E]
    idx7 = np.random.permutation(O)[:E]
    fk = mx_kscale(K)
    fr = mx_kscale(R)
    fl = mx_kscale(L)
    xtp = pack_weight(n((K, T)) / fk[:, None], "e2m1")
    xop = pack_weight(n((K, Z)) / fk[:, None], "e4m3")
    wp = pack_weight(n((K, R)) * 1 / np.sqrt(K) * fk[:, None] * fr, "e4m3")
    w2p = pack_weight(n((K, R)) * 1 / np.sqrt(K) * fk[:, None] * fr, "e5m2")
    wbp = pack_weight(n((R, N)) * 1 / np.sqrt(R) / fr[:, None], "e2m1")
    sxp = pack_weight(n((L, O)) / fl[:, None], "e4m3")
    wsp = pack_weight(n((L, N)) * 1 / np.sqrt(L) * fl[:, None], "e4m3")
    return {
        "xt_words": xtp[0],
        "xt_scales": xtp[1],
        "xo_words": xop[0],
        "xo_scales": xop[1],
        "w_words": wp[0],
        "w_scales": wp[1],
        "w2_words": w2p[0],
        "w2_scales": w2p[1],
        "wb_words": wbp[0],
        "wb_scales": wbp[1],
        "sx_words": sxp[0],
        "sx_scales": sxp[1],
        "ws_words": wsp[0],
        "ws_scales": wsp[1],
        "offs": striped(idx),
        "offs2": striped(idx2),
        "offs3": striped(idx3),
        "offs4": striped(idx4),
        "offs5": striped(idx5),
        "offs6": striped(idx6),
        "offs7": striped(idx7),
    }


def reference(xt_words, xt_scales, xo_words, xo_scales, w_words, w_scales, w2_words, w2_scales, wb_words, wb_scales, sx_words, sx_scales, ws_words, ws_scales, offs, offs2, offs3, offs4, offs5, offs6, offs7):
    idx = unstriped(offs)
    idx2 = unstriped(offs2)
    idx3 = unstriped(offs3)
    idx4 = unstriped(offs4)
    idx5 = unstriped(offs5)
    idx6 = unstriped(offs6)
    idx7 = unstriped(offs7)
    xtu = unpack_weight(xt_words, xt_scales, "e2m1")
    xou = unpack_weight(xo_words, xo_scales, "e4m3")
    wu = unpack_weight(w_words, w_scales, "e4m3")
    w2u = unpack_weight(w2_words, w2_scales, "e5m2")
    wbu = unpack_weight(wb_words, wb_scales, "e2m1")
    sxu = unpack_weight(sx_words, sx_scales, "e4m3")
    wsu = unpack_weight(ws_words, ws_scales, "e4m3")
    xtidxg = xtu[:, idx]
    xoidx2g = xou[:, idx2]
    a = wu.T @ xtidxg + w2u.T @ xoidx2g
    b = w2u.T @ xtidxg + wu.T @ xoidx2g
    pw = np.zeros((R, C))
    pw[:, idx3] = a
    pv = np.zeros((R, C))
    pv[:, idx4] = b
    pg = pw + pv
    hid = pg[:, idx5]
    hidq = mxq(hid, 0, "e5m2")
    p = wbu.T @ hidq + wsu.T @ sxu
    y = np.maximum(p[:, idx6], p[:, idx7])
    return y

@@ -1,0 +1,208 @@
+from contextlib import ExitStack
+
+import concourse.mybir as mybir
+
+K, T, Z, J, R, C, O, N, L, E = 512, 1024, 1024, 256, 512, 512, 256, 256, 512, 128
+FLOPS = 4 * 2 * K * R * J + 2 * R * N * O + 2 * L * N * O
+
+F32 = mybir.dt.float32
+BF16 = mybir.dt.bfloat16
+I32 = mybir.dt.int32
+U32 = mybir.dt.uint32
+U16 = mybir.dt.uint16
+U8 = mybir.dt.uint8
+E4M3 = mybir.dt.float8_e4m3fn_x4
+E5M2 = mybir.dt.float8_e5m2_x4
+E2M1 = mybir.dt.float4_e2m1fn_x4
+COPY = mybir.ActivationFunctionType.Copy
+ADD = mybir.AluOpType.add
+MAX = mybir.AluOpType.max
+
+P = 128
+PACK = 4
+QUADS = 4
+QUAD = 32
+ROWS = 4
+
+
+def load_scales(queue, dst, scales):
+    queue.dma_start(out=dst[0 : QUADS * ROWS, :].bitcast(I32), in_=scales[0].bitcast(I32))
+
+
+def load_words8(queue, dst, words):
+    queue.dma_start(out=dst[:].bitcast(I32), in_=words[0].rearrange("p c t -> p (c t)").bitcast(I32))
+
+
+def load_words4(queue, dst, words):
+    queue.dma_start(out=dst[:].bitcast(I32), in_=words[0].bitcast(I32))
+
+
+def tile_list_crossed_shared_skip_bestoftwo_kernel(
+    tc, xt_words, xt_scales, xo_words, xo_scales, w_words, w_scales, w2_words, w2_scales,
+    wb_words, wb_scales, sx_words, sx_scales, ws_words, ws_scales,
+    offs, offs2, offs3, offs4, offs5, offs6, offs7, out,
+):
+    nc = tc.nc
+    with ExitStack() as ctx:
+        lists = ctx.enter_context(tc.tile_pool(name="lists", bufs=1))
+        sb = ctx.enter_context(tc.tile_pool(name="sb", bufs=1))
+        psum = ctx.enter_context(tc.psum_pool(name="psum", bufs=1))
+
+        def list_tile(name, n):
+            return lists.tile([P, n // 16], U16, name=name)
+
+        def held(name, shape, dtype):
+            return sb.tile([P] + shape, dtype, name=name, align_bytes=64)
+
+        idx, idx2 = list_tile("idx", J), list_tile("idx2", J)
+        idx3, idx4, idx5 = list_tile("idx3", J), list_tile("idx4", J), list_tile("idx5", O)
+        idx6, idx7 = list_tile("idx6", E), list_tile("idx7", E)
+
+        xt_w, xt_s = held("xt_w", [T], U16), held("xt_s", [T], U8)
+        xo_w, xo_s = held("xo_w", [Z], U32), held("xo_s", [Z], U8)
+        w_raw, w2_raw = held("w_raw", [R], U32), held("w2_raw", [R], U32)
+        raw_s = held("raw_s", [2 * R], U8)
+        wb_w, sx_w, ws_w = held("wb_w", [2 * N], U8), held("sx_w", [O], U32), held("ws_w", [N], U32)
+
+        widths = (R, R, J, J, N, O, N)
+        starts = [sum(widths[:n]) for n in range(len(widths) + 1)]
+        planes = held("planes", [starts[-1]], U8)
+        w_s, w2_s, tok_s, note_s, wb_s, sx_s, ws_s = [planes[:, starts[n] : starts[n + 1]] for n in range(len(widths))]
+
+        nc.vector.memset(xt_s[:].bitcast(I32), 0)
+        nc.vector.memset(xo_s[:].bitcast(I32), 0)
+        nc.vector.memset(raw_s[:].bitcast(I32), 0)
+        nc.vector.memset(planes[:, starts[4] :].bitcast(I32), 0)
+
+        nc.sync.dma_start(idx[:], offs)
+        nc.sync.dma_start(idx2[:], offs2)
+        load_scales(nc.scalar, xt_s[:], xt_scales)
+        load_scales(nc.scalar, xo_s[:], xo_scales)
+        load_scales(nc.scalar, raw_s[:, 0:R], w_scales)
+        load_scales(nc.scalar, raw_s[:, R : 2 * R], w2_scales)
+        load_words8(nc.sync, w_raw, w_words)
+        load_words8(nc.sync, w2_raw, w2_words)
+        load_words4(nc.sync, xt_w, xt_words)
+        load_words8(nc.sync, xo_w, xo_words)
+        load_scales(nc.sync, wb_s, wb_scales)
+        load_scales(nc.sync, sx_s, sx_scales)
+        load_scales(nc.sync, ws_s, ws_scales)
+        nc.sync.dma_start(idx3[:], offs3)
+        nc.sync.dma_start(idx4[:], offs4)
+        nc.sync.dma_start(idx5[:], offs5)
+        load_words8(nc.sync, ws_w, ws_words)
+        load_words8(nc.sync, sx_w, sx_words)
+        load_words4(nc.sync, wb_w, wb_words)
+        nc.sync.dma_start(idx6[:], offs6)
+        nc.sync.dma_start(idx7[:], offs7)
+
+        pw = [held("pw%d" % n, [C], F32) for n in range(2)]
+        pv = [held("pv%d" % n, [C], F32) for n in range(2)]
+        for n in range(2):
+            nc.vector.memset(pw[n][:], 0.0)
+            nc.vector.memset(pv[n][:], 0.0)
+
+        def deal(dst, src, run):
+            nc.vector.tensor_copy(
+                out=dst.rearrange("p (t c i) -> p c t i", t=PACK, i=run),
+                in_=src.rearrange("p (c i t) -> p c t i", t=PACK, i=run),
+            )
+
+        w_w, w2_w = held("w_w", [R], U32), held("w2_w", [R], U32)
+        xtg_w, xtg_s = held("xtg_w", [J], U16), held("xtg_s", [J], U8)
+        xog_w, xog_s = held("xog_w", [J], U32), held("xog_s", [J], U8)
+
+        nc.vector.tensor_copy(xtg_s[:], xt_s[:].indirect(idx[:]))
+        nc.vector.tensor_copy(xog_s[:], xo_s[:].indirect(idx2[:]))
+        deal(w_s, raw_s[:, 0:R], 16)
+        nc.vector.tensor_copy(tok_s.bitcast(I32), xtg_s[:].bitcast(I32))
+        nc.vector.tensor_copy(note_s.bitcast(I32), xog_s[:].bitcast(I32))
+        deal(w2_s, raw_s[:, R : 2 * R], 16)
+        for q in range(1, QUADS):
+            nc.scalar.dma_start(
+                out=planes[QUAD * q : QUAD * q + ROWS, :].bitcast(I32),
+                in_=planes[ROWS * q : ROWS * q + ROWS, :].bitcast(I32),
+            )
+        deal(w_w[:], w_raw[:], 4)
+        deal(w2_w[:], w2_raw[:], 4)
+        nc.vector.tensor_copy(xtg_w[:], xt_w[:].indirect(idx[:]))
+        nc.vector.tensor_copy(xog_w[:], xo_w[:].indirect(idx2[:]))
+
+        first = (w_w, w_s, E4M3)
+        second = (w2_w, w2_s, E5M2)
+        tokens = (xtg_w[:].bitcast(E2M1), tok_s)
+        notes = (xog_w[:].bitcast(E4M3), note_s)
+
+        def stage_one(name, t, on_tokens, on_notes):
+            acc = psum.tile([P, J], F32, name=name, tag=name)
+            cols = slice(t * P, (t + 1) * P)
+            for (words, scales, fmt), (rhs, rhs_scale), start in ((on_tokens, tokens, True), (on_notes, notes, False)):
+                nc.tensor.matmul_mx(
+                    out=acc[:], lhsT=words[:, cols].bitcast(fmt), lhsT_scale=scales[:, cols],
+                    rhs=rhs, rhs_scale=rhs_scale, start=start, stop=not start,
+                )
+            return acc
+
+        a_ps, b_ps = [], []
+        for t in range(PACK):
+            a_ps.append(stage_one("bank_a%d" % t, t, first, second))
+            b_ps.append(stage_one("bank_b%d" % t, t, second, first))
+
+        a_sb = [held("a%d" % t, [J], F32) for t in range(PACK)]
+        b_sb = [held("b%d" % t, [J], F32) for t in range(PACK)]
+        pg = [held("pg%d" % t, [C], F32) for t in range(PACK)]
+        hid_rows = held("hid_rows", [PACK, O], BF16)
+        last = PACK - 1
+        half = O // 2
+
+        nc.vector.tensor_copy(a_sb[0][:], a_ps[0][:])
+        nc.scalar.copy(b_sb[0][:], b_ps[0][:])
+        for t in range(PACK):
+            nc.vector.tensor_copy(pw[t % 2][:].indirect(idx3[:]), a_sb[t][:])
+            nc.scalar.activation(pv[t % 2][:].indirect(idx4[:]), b_sb[t][:], COPY)
+            if t > 0:
+                nc.scalar.activation(hid_rows[:, t - 1, :], pg[t - 1][:].indirect(idx5[:]), COPY)
+            if t < last:
+                nc.vector.tensor_copy(a_sb[t + 1][:], a_ps[t + 1][:])
+                nc.scalar.copy(b_sb[t + 1][:], b_ps[t + 1][:])
+            nc.vector.tensor_tensor(pg[t][:], pw[t % 2][:], pv[t % 2][:], ADD)
+        nc.vector.tensor_copy(hid_rows[:, last, 0:half], pg[last][:].indirect(idx5[:, 0 : half // 16]))
+        nc.scalar.activation(hid_rows[:, last, half:O], pg[last][:].indirect(idx5[:, half // 16 : O // 16]), COPY)
+
+        hid = held("hid", [O * PACK], BF16)
+        nc.vector.tensor_copy(
+            out=hid[:].rearrange("p (c i t) -> p c t i", t=PACK, i=4),
+            in_=hid_rows[:].rearrange("p t (c i) -> p c t i", i=4),
+        )
+        hid_w, hid_s = held("hid_w", [O], U32), held("hid_s", [O], U8)
+        nc.vector.quantize_mx(out=hid_w[:].bitcast(E5M2), scales=hid_s[:], in_=hid[:])
+
+        p_ps = []
+        for h, bank in enumerate(("bank_a0", "bank_b0")):
+            acc = psum.tile([P, O], F32, name="p%d" % h, tag=bank)
+            cols = slice(h * P, (h + 1) * P)
+            nc.tensor.matmul_mx(
+                out=acc[:], lhsT=ws_w[:, cols].bitcast(E4M3), lhsT_scale=ws_s[:, cols],
+                rhs=sx_w[:].bitcast(E4M3), rhs_scale=sx_s, start=True, stop=False,
+            )
+            p_ps.append(acc)
+        for h in range(2):
+            cols = slice(h * P, (h + 1) * P)
+            nc.tensor.matmul_mx(
+                out=p_ps[h][:], lhsT=wb_w[:, 2 * h * P : 2 * (h + 1) * P].bitcast(E2M1), lhsT_scale=wb_s[:, cols],
+                rhs=hid_w[:].bitcast(E5M2), rhs_scale=hid_s[:], start=False, stop=True,
+            )
+
+        p_sb = [held("p_sb%d" % h, [O], F32) for h in range(2)]
+        left = [held("left%d" % h, [E], F32) for h in range(2)]
+        right = [held("right%d" % h, [E], F32) for h in range(2)]
+        best = [held("best%d" % h, [E], F32) for h in range(2)]
+        nc.vector.tensor_copy(p_sb[0][:], p_ps[0][:])
+        nc.scalar.copy(p_sb[1][:], p_ps[1][:])
+        nc.vector.tensor_copy(left[0][:], p_sb[0][:].indirect(idx6[:]))
+        nc.vector.tensor_copy(right[0][:], p_sb[0][:].indirect(idx7[:]))
+        nc.scalar.activation(left[1][:], p_sb[1][:].indirect(idx6[:]), COPY)
+        nc.scalar.activation(right[1][:], p_sb[1][:].indirect(idx7[:]), COPY)
+        for h in range(2):
+            nc.vector.tensor_tensor(best[h][:], left[h][:], right[h][:], MAX)
+            nc.sync.dma_start(out=out[h * P : (h + 1) * P, :], in_=best[h][:])

@@ -23,18 +23,44 @@ PACK = 4
 QUADS = 4
 QUAD = 32
 ROWS = 4
+TWICE = 2
 
 
 def load_scales(queue, dst, scales):
-    queue.dma_start(out=dst[0 : QUADS * ROWS, :].bitcast(I32), in_=scales[0].bitcast(I32))
+    rows = scales[0].bitcast(I32)
+    queue.dma_start(
+        out=dst[0:QUAD, :].bitcast(I32),
+        in_=rows.unsqueeze(1).broadcast_to([QUADS * ROWS, TWICE, rows.shape[1]]),
+    )
+
+
+def clear_rest(engine, dst):
+    engine.memset(dst[QUAD : 2 * QUAD, :].bitcast(I32), 0)
+    engine.memset(dst[2 * QUAD : P, :].bitcast(I32), 0)
+
+
+def place_scales(queue, dst, src):
+    span = TWICE * ROWS
+    for q in range(QUADS):
+        queue.dma_start(
+            out=dst[QUAD * q : QUAD * q + ROWS, :].bitcast(I32),
+            in_=src[span * q : span * (q + 1) : TWICE, :].bitcast(I32),
+        )
 
 
 def load_words8(queue, dst, words):
-    queue.dma_start(out=dst[:].bitcast(I32), in_=words[0].rearrange("p c t -> p (c t)").bitcast(I32))
+    queue.dma_start(out=dst.bitcast(I32), in_=words[0].rearrange("p c t -> p (c t)").bitcast(I32))
 
 
 def load_words4(queue, dst, words):
-    queue.dma_start(out=dst[:].bitcast(I32), in_=words[0].bitcast(I32))
+    queue.dma_start(out=dst.bitcast(I32), in_=words[0].bitcast(I32))
+
+
+def deal(move, dst, src, run):
+    move(
+        out=dst.rearrange("p (t c i) -> p c t i", t=PACK, i=run),
+        in_=src.rearrange("p (c i t) -> p c t i", t=PACK, i=run),
+    )
 
 
 def tile_list_crossed_shared_skip_bestoftwo_kernel(
@@ -46,67 +72,49 @@ def tile_list_crossed_shared_skip_bestoftwo_kernel(
     with ExitStack() as ctx:
         lists = ctx.enter_context(tc.tile_pool(name="lists", bufs=1))
         sb = ctx.enter_context(tc.tile_pool(name="sb", bufs=1))
+        reuse = ctx.enter_context(tc.tile_pool(name="reuse", bufs=1))
         psum = ctx.enter_context(tc.psum_pool(name="psum", bufs=1))
 
         def list_tile(name, n):
             return lists.tile([P, n // 16], U16, name=name)
 
-        def held(name, shape, dtype):
-            return sb.tile([P] + shape, dtype, name=name, align_bytes=64)
+        def held(name, shape, dtype, tag=None):
+            return sb.tile([P] + shape, dtype, name=name, tag=tag or name, align_bytes=64)
 
         idx, idx2 = list_tile("idx", J), list_tile("idx2", J)
         idx3, idx4, idx5 = list_tile("idx3", J), list_tile("idx4", J), list_tile("idx5", O)
         idx6, idx7 = list_tile("idx6", E), list_tile("idx7", E)
 
         xt_w, xt_s = held("xt_w", [T], U16), held("xt_s", [T], U8)
-        xo_w, xo_s = held("xo_w", [Z], U32), held("xo_s", [Z], U8)
+        rest = (PACK - 1) * 2 * P
+        xo_w = reuse.tile([P, Z], U32, name="xo_w", offset=0, align_bytes=64)
+        xo_s = held("xo_s", [Z], U8)
         w_raw, w2_raw = held("w_raw", [R], U32), held("w2_raw", [R], U32)
         raw_s = held("raw_s", [2 * R], U8)
-        wb_w, sx_w, ws_w = held("wb_w", [2 * N], U8), held("sx_w", [O], U32), held("ws_w", [N], U32)
-
-        widths = (R, R, J, J, N, O, N)
-        starts = [sum(widths[:n]) for n in range(len(widths) + 1)]
-        planes = held("planes", [starts[-1]], U8)
-        w_s, w2_s, tok_s, note_s, wb_s, sx_s, ws_s = [planes[:, starts[n] : starts[n + 1]] for n in range(len(widths))]
-
-        nc.vector.memset(xt_s[:].bitcast(I32), 0)
-        nc.vector.memset(xo_s[:].bitcast(I32), 0)
-        nc.vector.memset(raw_s[:].bitcast(I32), 0)
-        nc.vector.memset(planes[:, starts[4] :].bitcast(I32), 0)
 
         nc.sync.dma_start(idx[:], offs)
-        nc.sync.dma_start(idx2[:], offs2)
         load_scales(nc.scalar, xt_s[:], xt_scales)
+        nc.sync.dma_start(idx2[:], offs2)
         load_scales(nc.scalar, xo_s[:], xo_scales)
-        load_scales(nc.scalar, raw_s[:, 0:R], w_scales)
+        load_scales(nc.sync, raw_s[:, 0:R], w_scales)
         load_scales(nc.scalar, raw_s[:, R : 2 * R], w2_scales)
-        load_words8(nc.sync, w_raw, w_words)
-        load_words8(nc.sync, w2_raw, w2_words)
-        load_words4(nc.sync, xt_w, xt_words)
-        load_words8(nc.sync, xo_w, xo_words)
-        load_scales(nc.sync, wb_s, wb_scales)
-        load_scales(nc.sync, sx_s, sx_scales)
-        load_scales(nc.sync, ws_s, ws_scales)
+        load_words8(nc.sync, xo_w[:], xo_words)
+        load_words4(nc.scalar, xt_w[:], xt_words)
         nc.sync.dma_start(idx3[:], offs3)
         nc.sync.dma_start(idx4[:], offs4)
         nc.sync.dma_start(idx5[:], offs5)
-        load_words8(nc.sync, ws_w, ws_words)
-        load_words8(nc.sync, sx_w, sx_words)
-        load_words4(nc.sync, wb_w, wb_words)
-        nc.sync.dma_start(idx6[:], offs6)
-        nc.sync.dma_start(idx7[:], offs7)
+        load_words8(nc.sync, w_raw[:], w_words)
+        load_words8(nc.sync, w2_raw[:], w2_words)
 
-        pw = [held("pw%d" % n, [C], F32) for n in range(2)]
-        pv = [held("pv%d" % n, [C], F32) for n in range(2)]
-        for n in range(2):
-            nc.vector.memset(pw[n][:], 0.0)
-            nc.vector.memset(pv[n][:], 0.0)
-
-        def deal(dst, src, run):
-            nc.vector.tensor_copy(
-                out=dst.rearrange("p (t c i) -> p c t i", t=PACK, i=run),
-                in_=src.rearrange("p (c i t) -> p c t i", t=PACK, i=run),
-            )
+        early = 2 * R + 2 * J
+        planes = held("planes", [early], U8)
+        tok_s, note_s = planes[:, 0:J], planes[:, J : 2 * J]
+        pair = 2 * P
+        lead = 2 * J + pair
+        rows = held("rows", [lead], U8, tag="xo_s")
+        for staged in (xt_s, xo_s, raw_s):
+            clear_rest(nc.vector, staged)
+        nc.gpsimd.memset(planes[:].bitcast(I32), 0)
 
         w_w, w2_w = held("w_w", [R], U32), held("w2_w", [R], U32)
         xtg_w, xtg_s = held("xtg_w", [J], U16), held("xtg_s", [J], U8)
@@ -114,84 +122,121 @@ def tile_list_crossed_shared_skip_bestoftwo_kernel(
 
         nc.vector.tensor_copy(xtg_s[:], xt_s[:].indirect(idx[:]))
         nc.vector.tensor_copy(xog_s[:], xo_s[:].indirect(idx2[:]))
-        deal(w_s, raw_s[:, 0:R], 16)
-        nc.vector.tensor_copy(tok_s.bitcast(I32), xtg_s[:].bitcast(I32))
-        nc.vector.tensor_copy(note_s.bitcast(I32), xog_s[:].bitcast(I32))
-        deal(w2_s, raw_s[:, R : 2 * R], 16)
-        for q in range(1, QUADS):
-            nc.scalar.dma_start(
-                out=planes[QUAD * q : QUAD * q + ROWS, :].bitcast(I32),
-                in_=planes[ROWS * q : ROWS * q + ROWS, :].bitcast(I32),
-            )
-        deal(w_w[:], w_raw[:], 4)
-        deal(w2_w[:], w2_raw[:], 4)
+        nc.vector.tensor_copy(rows[:, 0:J].bitcast(I32), xtg_s[:].bitcast(I32))
+        nc.vector.tensor_copy(rows[:, J : 2 * J].bitcast(I32), xog_s[:].bitcast(I32))
+        nc.vector.tensor_copy(rows[:, 2 * J : lead], raw_s[:, 0 : 2 * R : PACK])
+        place_scales(nc.sync, planes[:, 0:lead], rows[:])
+        rest_rows = held("rest_rows", [rest], U8)
+        nc.vector.tensor_copy(
+            out=rest_rows[:].rearrange("p (t c i) -> p c t i", t=PACK - 1, i=16),
+            in_=raw_s[:].rearrange("p (c i t) -> p c t i", t=PACK, i=16)[:, :, 1:PACK, :],
+        )
+        place_scales(nc.sync, planes[:, lead:], rest_rows[:])
+        nc.sync.dma_start(idx6[:], offs6)
+        nc.sync.dma_start(idx7[:], offs7)
         nc.vector.tensor_copy(xtg_w[:], xt_w[:].indirect(idx[:]))
         nc.vector.tensor_copy(xog_w[:], xo_w[:].indirect(idx2[:]))
+        deal(nc.scalar.copy, w_w[:], w_raw[:], 4)
+        deal(nc.scalar.copy, w2_w[:], w2_raw[:], 4)
 
-        first = (w_w, w_s, E4M3)
-        second = (w2_w, w2_s, E5M2)
+        pv0 = reuse.tile([P, C], F32, name="pv0", offset=0, align_bytes=64)
+        pw0 = reuse.tile([P, C], F32, name="pw0", offset=4 * C, align_bytes=64)
+        pw = [pw0, held("pw1", [C], F32, tag="w2_raw")]
+        pv = [pv0, held("pv1", [C], F32, tag="w_raw")]
+        for board in (pv[0], pw[0], pv[1], pw[1]):
+            nc.vector.memset(board[:], 0.0)
+
+        late = N + O + N
+        late_rows = held("late_rows", [late], U8, tag="raw_s")
+        late_planes = held("late_planes", [late], U8)
+        wb_s, sx_s, ws_s = late_planes[:, 0:N], late_planes[:, N : N + O], late_planes[:, N + O :]
+        late_w = held("late_w", [N + O + N // 2], U32, tag="xo_s")
+        ws_w, sx_w, wb_w = late_w[:, 0:N], late_w[:, N : N + O], late_w[:, N + O :]
+        nc.gpsimd.memset(late_planes[:].bitcast(I32), 0)
+        load_scales(nc.sync, late_rows[:, 0:N], wb_scales)
+        load_scales(nc.sync, late_rows[:, N : N + O], sx_scales)
+        load_scales(nc.sync, late_rows[:, N + O :], ws_scales)
+        load_words8(nc.sync, ws_w, ws_words)
+        load_words8(nc.sync, sx_w, sx_words)
+        load_words4(nc.sync, wb_w, wb_words)
+        place_scales(nc.sync, late_planes, late_rows[:, 0:late])
+
+        first = (w_w, 0, E4M3)
+        second = (w2_w, 1, E5M2)
         tokens = (xtg_w[:].bitcast(E2M1), tok_s)
         notes = (xog_w[:].bitcast(E4M3), note_s)
 
-        def stage_one(name, t, on_tokens, on_notes):
-            acc = psum.tile([P, J], F32, name=name, tag=name)
+        def stage_one(acc, t, on_tokens, on_notes):
             cols = slice(t * P, (t + 1) * P)
-            for (words, scales, fmt), (rhs, rhs_scale), start in ((on_tokens, tokens, True), (on_notes, notes, False)):
+            for (words, which, fmt), (rhs, rhs_scale), start in ((on_tokens, tokens, True), (on_notes, notes, False)):
+                at = 2 * J + t * pair + which * P
                 nc.tensor.matmul_mx(
-                    out=acc[:], lhsT=words[:, cols].bitcast(fmt), lhsT_scale=scales[:, cols],
+                    out=acc, lhsT=words[:, cols].bitcast(fmt), lhsT_scale=planes[:, at : at + P],
                     rhs=rhs, rhs_scale=rhs_scale, start=start, stop=not start,
                 )
-            return acc
 
-        a_ps, b_ps = [], []
-        for t in range(PACK):
-            a_ps.append(stage_one("bank_a%d" % t, t, first, second))
-            b_ps.append(stage_one("bank_b%d" % t, t, second, first))
-
-        a_sb = [held("a%d" % t, [J], F32) for t in range(PACK)]
-        b_sb = [held("b%d" % t, [J], F32) for t in range(PACK)]
-        pg = [held("pg%d" % t, [C], F32) for t in range(PACK)]
-        hid_rows = held("hid_rows", [PACK, O], BF16)
         last = PACK - 1
+        a_ps, b_ps = [], []
+        for t in range(last):
+            b_ps.append(psum.tile([P, J], F32, name="b%d_ps" % t))
+            a_ps.append(psum.tile([P, J], F32, name="a%d_ps" % t))
+            stage_one(b_ps[t][:], t, second, first)
+            stage_one(a_ps[t][:], t, first, second)
+        last_ps = psum.tile([P, 2 * J], F32, name="last_ps")
+        stage_one(last_ps[:, 0:J], last, first, second)
+        stage_one(last_ps[:, J:], last, second, first)
+
+        a_sb = [held("a%d" % t, [J], F32)[:] for t in range(last)]
+        b_sb = [held("b%d" % t, [J], F32)[:] for t in range(last)]
+        last_sb = held("last_sb", [2 * J], F32)
+        a_sb.append(last_sb[:, 0:J])
+        b_sb.append(last_sb[:, J:])
+        pg = [held("pg%d" % t, [C], F32) for t in range(PACK)]
+        hid_rows = held("hid_rows", [PACK, O], BF16, tag="b1")
         half = O // 2
 
-        nc.vector.tensor_copy(a_sb[0][:], a_ps[0][:])
-        nc.scalar.copy(b_sb[0][:], b_ps[0][:])
         for t in range(PACK):
-            nc.vector.tensor_copy(pw[t % 2][:].indirect(idx3[:]), a_sb[t][:])
-            nc.scalar.activation(pv[t % 2][:].indirect(idx4[:]), b_sb[t][:], COPY)
+            for ahead in ((0,), (1, 2), (), ())[t]:
+                nc.scalar.copy(b_sb[ahead], b_ps[ahead][:])
+                nc.vector.tensor_copy(a_sb[ahead], a_ps[ahead][:])
+            if t + 1 == last:
+                nc.vector.tensor_copy(last_sb[:], last_ps[:])
+            nc.vector.tensor_copy(pw[t % 2][:].indirect(idx3[:]), a_sb[t])
+            nc.scalar.activation(pv[t % 2][:].indirect(idx4[:]), b_sb[t], COPY)
             if t > 0:
                 nc.scalar.activation(hid_rows[:, t - 1, :], pg[t - 1][:].indirect(idx5[:]), COPY)
-            if t < last:
-                nc.vector.tensor_copy(a_sb[t + 1][:], a_ps[t + 1][:])
-                nc.scalar.copy(b_sb[t + 1][:], b_ps[t + 1][:])
-            nc.vector.tensor_tensor(pg[t][:], pw[t % 2][:], pv[t % 2][:], ADD)
+            adder = nc.gpsimd if t < last else nc.vector
+            adder.tensor_tensor(pg[t][:], pw[t % 2][:], pv[t % 2][:], ADD)
         nc.vector.tensor_copy(hid_rows[:, last, 0:half], pg[last][:].indirect(idx5[:, 0 : half // 16]))
         nc.scalar.activation(hid_rows[:, last, half:O], pg[last][:].indirect(idx5[:, half // 16 : O // 16]), COPY)
 
-        hid = held("hid", [O * PACK], BF16)
-        nc.vector.tensor_copy(
-            out=hid[:].rearrange("p (c i t) -> p c t i", t=PACK, i=4),
-            in_=hid_rows[:].rearrange("p t (c i) -> p c t i", i=4),
-        )
-        hid_w, hid_s = held("hid_w", [O], U32), held("hid_s", [O], U8)
-        nc.vector.quantize_mx(out=hid_w[:].bitcast(E5M2), scales=hid_s[:], in_=hid[:])
+        hid = [held("hid%d" % u, [half * PACK], BF16) for u in range(2)]
+        hid_w = [held("hid_w%d" % u, [half], U32) for u in range(2)]
+        hid_s = [held("hid_s%d" % u, [half], U8) for u in range(2)]
+        for u, weave in enumerate((nc.vector.tensor_copy, nc.scalar.copy)):
+            weave(
+                out=hid[u][:].rearrange("p (c i t) -> p c t i", t=PACK, i=4),
+                in_=hid_rows[:, :, u * half : (u + 1) * half].rearrange("p t (c i) -> p c t i", i=4),
+            )
+            nc.vector.quantize_mx(out=hid_w[u][:].bitcast(E5M2), scales=hid_s[u][:], in_=hid[u][:])
 
         p_ps = []
-        for h, bank in enumerate(("bank_a0", "bank_b0")):
-            acc = psum.tile([P, O], F32, name="p%d" % h, tag=bank)
+        for h, bank in enumerate(("b0_ps", "p1_ps")):
+            acc = psum.tile([P, O], F32, name="p%d_ps" % h, tag=bank)
             cols = slice(h * P, (h + 1) * P)
             nc.tensor.matmul_mx(
                 out=acc[:], lhsT=ws_w[:, cols].bitcast(E4M3), lhsT_scale=ws_s[:, cols],
-                rhs=sx_w[:].bitcast(E4M3), rhs_scale=sx_s, start=True, stop=False,
+                rhs=sx_w.bitcast(E4M3), rhs_scale=sx_s, start=True, stop=False,
             )
             p_ps.append(acc)
-        for h in range(2):
-            cols = slice(h * P, (h + 1) * P)
-            nc.tensor.matmul_mx(
-                out=p_ps[h][:], lhsT=wb_w[:, 2 * h * P : 2 * (h + 1) * P].bitcast(E2M1), lhsT_scale=wb_s[:, cols],
-                rhs=hid_w[:].bitcast(E5M2), rhs_scale=hid_s[:], start=False, stop=True,
-            )
+        for u in range(2):
+            for h in range(2):
+                cols = slice(h * P, (h + 1) * P)
+                nc.tensor.matmul_mx(
+                    out=p_ps[h][:, u * half : (u + 1) * half],
+                    lhsT=wb_w.bitcast(E2M1)[:, cols], lhsT_scale=wb_s[:, cols],
+                    rhs=hid_w[u][:].bitcast(E5M2), rhs_scale=hid_s[u][:], start=False, stop=(u == 1),
+                )
 
         p_sb = [held("p_sb%d" % h, [O], F32) for h in range(2)]
         left = [held("left%d" % h, [E], F32) for h in range(2)]

@@ -20,31 +20,39 @@ MAX = mybir.AluOpType.max
 
 P = 128
 PACK = 4
-QUADS = 4
 QUAD = 32
-ROWS = 4
-TWICE = 2
+QUADS = P // QUAD
+QUAD_ROWS = 4
+SCALE_ROWS = QUADS * QUAD_ROWS
+TWICE = QUAD // SCALE_ROWS
+LIST_ROWS = 16
+LINE = 16
+HALVES = 2
 
 
-def load_scales(queue, dst, scales):
+def load_scales_twice(queue, dst, scales):
     rows = scales[0].bitcast(I32)
     queue.dma_start(
         out=dst[0:QUAD, :].bitcast(I32),
-        in_=rows.unsqueeze(1).broadcast_to([QUADS * ROWS, TWICE, rows.shape[1]]),
+        in_=rows.unsqueeze(1).broadcast_to([SCALE_ROWS, TWICE, rows.shape[1]]),
     )
 
 
-def clear_rest(engine, dst):
+def clear_upper_quadrants(engine, dst):
     engine.memset(dst[QUAD : 2 * QUAD, :].bitcast(I32), 0)
     engine.memset(dst[2 * QUAD : P, :].bitcast(I32), 0)
 
 
-def place_scales(queue, dst, src):
-    span = TWICE * ROWS
+def load_scales(queue, dst, scales):
+    queue.dma_start(out=dst[0:SCALE_ROWS, :].bitcast(I32), in_=scales[0].bitcast(I32))
+
+
+def place_scales(queue, planes, staged, step):
+    span = step * QUAD_ROWS
     for q in range(QUADS):
         queue.dma_start(
-            out=dst[QUAD * q : QUAD * q + ROWS, :].bitcast(I32),
-            in_=src[span * q : span * (q + 1) : TWICE, :].bitcast(I32),
+            out=planes[QUAD * q : QUAD * q + QUAD_ROWS, :].bitcast(I32),
+            in_=staged[span * q : span * (q + 1) : step, :].bitcast(I32),
         )
 
 
@@ -72,11 +80,10 @@ def tile_list_crossed_shared_skip_bestoftwo_kernel(
     with ExitStack() as ctx:
         lists = ctx.enter_context(tc.tile_pool(name="lists", bufs=1))
         sb = ctx.enter_context(tc.tile_pool(name="sb", bufs=1))
-        reuse = ctx.enter_context(tc.tile_pool(name="reuse", bufs=1))
         psum = ctx.enter_context(tc.psum_pool(name="psum", bufs=1))
 
-        def list_tile(name, n):
-            return lists.tile([P, n // 16], U16, name=name)
+        def list_tile(name, entries):
+            return lists.tile([P, entries // LIST_ROWS], U16, name=name)
 
         def held(name, shape, dtype, tag=None):
             return sb.tile([P] + shape, dtype, name=name, tag=tag or name, align_bytes=64)
@@ -86,18 +93,16 @@ def tile_list_crossed_shared_skip_bestoftwo_kernel(
         idx6, idx7 = list_tile("idx6", E), list_tile("idx7", E)
 
         xt_w, xt_s = held("xt_w", [T], U16), held("xt_s", [T], U8)
-        rest = (PACK - 1) * 2 * P
-        xo_w = reuse.tile([P, Z], U32, name="xo_w", offset=0, align_bytes=64)
-        xo_s = held("xo_s", [Z], U8)
+        xo_w, xo_s = held("xo_w", [Z], U32), held("xo_s", [Z], U8)
         w_raw, w2_raw = held("w_raw", [R], U32), held("w2_raw", [R], U32)
         raw_s = held("raw_s", [2 * R], U8)
 
         nc.sync.dma_start(idx[:], offs)
-        load_scales(nc.scalar, xt_s[:], xt_scales)
+        load_scales_twice(nc.scalar, xo_s[:], xo_scales)
         nc.sync.dma_start(idx2[:], offs2)
-        load_scales(nc.scalar, xo_s[:], xo_scales)
-        load_scales(nc.sync, raw_s[:, 0:R], w_scales)
-        load_scales(nc.scalar, raw_s[:, R : 2 * R], w2_scales)
+        load_scales_twice(nc.scalar, xt_s[:], xt_scales)
+        load_scales_twice(nc.sync, raw_s[:, 0:R], w_scales)
+        load_scales_twice(nc.scalar, raw_s[:, R : 2 * R], w2_scales)
         load_words8(nc.sync, xo_w[:], xo_words)
         load_words4(nc.scalar, xt_w[:], xt_words)
         nc.sync.dma_start(idx3[:], offs3)
@@ -106,14 +111,12 @@ def tile_list_crossed_shared_skip_bestoftwo_kernel(
         load_words8(nc.sync, w_raw[:], w_words)
         load_words8(nc.sync, w2_raw[:], w2_words)
 
-        early = 2 * R + 2 * J
-        planes = held("planes", [early], U8)
-        tok_s, note_s = planes[:, 0:J], planes[:, J : 2 * J]
-        pair = 2 * P
-        lead = 2 * J + pair
-        rows = held("rows", [lead], U8, tag="xo_s")
+        first_width = 2 * R + 2 * J
+        tok_cols, note_cols = slice(2 * R, 2 * R + J), slice(2 * R + J, first_width)
+        rows = held("rows", [first_width], U8)
+        planes = held("planes", [first_width], U8)
         for staged in (xt_s, xo_s, raw_s):
-            clear_rest(nc.vector, staged)
+            clear_upper_quadrants(nc.vector, staged)
         nc.gpsimd.memset(planes[:].bitcast(I32), 0)
 
         w_w, w2_w = held("w_w", [R], U32), held("w2_w", [R], U32)
@@ -122,35 +125,28 @@ def tile_list_crossed_shared_skip_bestoftwo_kernel(
 
         nc.vector.tensor_copy(xtg_s[:], xt_s[:].indirect(idx[:]))
         nc.vector.tensor_copy(xog_s[:], xo_s[:].indirect(idx2[:]))
-        nc.vector.tensor_copy(rows[:, 0:J].bitcast(I32), xtg_s[:].bitcast(I32))
-        nc.vector.tensor_copy(rows[:, J : 2 * J].bitcast(I32), xog_s[:].bitcast(I32))
-        nc.vector.tensor_copy(rows[:, 2 * J : lead], raw_s[:, 0 : 2 * R : PACK])
-        place_scales(nc.sync, planes[:, 0:lead], rows[:])
-        rest_rows = held("rest_rows", [rest], U8)
-        nc.vector.tensor_copy(
-            out=rest_rows[:].rearrange("p (t c i) -> p c t i", t=PACK - 1, i=16),
-            in_=raw_s[:].rearrange("p (c i t) -> p c t i", t=PACK, i=16)[:, :, 1:PACK, :],
-        )
-        place_scales(nc.sync, planes[:, lead:], rest_rows[:])
+        deal(nc.gpsimd.tensor_copy, rows[:, 0 : 2 * R], raw_s[:], LINE)
+        nc.vector.tensor_copy(rows[:, tok_cols].bitcast(I32), xtg_s[:].bitcast(I32))
+        nc.vector.tensor_copy(rows[:, note_cols].bitcast(I32), xog_s[:].bitcast(I32))
+        place_scales(nc.sync, planes, rows, TWICE)
         nc.sync.dma_start(idx6[:], offs6)
         nc.sync.dma_start(idx7[:], offs7)
-        nc.vector.tensor_copy(xtg_w[:], xt_w[:].indirect(idx[:]))
         nc.vector.tensor_copy(xog_w[:], xo_w[:].indirect(idx2[:]))
-        deal(nc.scalar.copy, w_w[:], w_raw[:], 4)
-        deal(nc.scalar.copy, w2_w[:], w2_raw[:], 4)
+        nc.vector.tensor_copy(xtg_w[:], xt_w[:].indirect(idx[:]))
+        deal(nc.scalar.copy, w_w[:], w_raw[:], LINE // 4)
+        deal(nc.scalar.copy, w2_w[:], w2_raw[:], LINE // 4)
 
-        pv0 = reuse.tile([P, C], F32, name="pv0", offset=0, align_bytes=64)
-        pw0 = reuse.tile([P, C], F32, name="pw0", offset=4 * C, align_bytes=64)
-        pw = [pw0, held("pw1", [C], F32, tag="w2_raw")]
-        pv = [pv0, held("pv1", [C], F32, tag="w_raw")]
-        for board in (pv[0], pw[0], pv[1], pw[1]):
-            nc.vector.memset(board[:], 0.0)
+        pw = [held("pw0", [C], F32, tag="xo_w"), held("pw1", [C], F32, tag="w2_raw")]
+        pv = [held("pv0", [C], F32, tag="xt_w"), held("pv1", [C], F32, tag="w_raw")]
+        for turn, engine in enumerate((nc.vector, nc.gpsimd)):
+            engine.memset(pv[turn][:], 0.0)
+            engine.memset(pw[turn][:], 0.0)
 
-        late = N + O + N
-        late_rows = held("late_rows", [late], U8, tag="raw_s")
-        late_planes = held("late_planes", [late], U8)
+        second_width = N + O + N
+        late_rows = held("late_rows", [second_width], U8, tag="raw_s")
+        late_planes = held("late_planes", [second_width], U8)
         wb_s, sx_s, ws_s = late_planes[:, 0:N], late_planes[:, N : N + O], late_planes[:, N + O :]
-        late_w = held("late_w", [N + O + N // 2], U32, tag="xo_s")
+        late_w = held("late_w", [N + O + N // 2], U32, tag="rows")
         ws_w, sx_w, wb_w = late_w[:, 0:N], late_w[:, N : N + O], late_w[:, N + O :]
         nc.gpsimd.memset(late_planes[:].bitcast(I32), 0)
         load_scales(nc.sync, late_rows[:, 0:N], wb_scales)
@@ -159,95 +155,104 @@ def tile_list_crossed_shared_skip_bestoftwo_kernel(
         load_words8(nc.sync, ws_w, ws_words)
         load_words8(nc.sync, sx_w, sx_words)
         load_words4(nc.sync, wb_w, wb_words)
-        place_scales(nc.sync, late_planes, late_rows[:, 0:late])
+        place_scales(nc.sync, late_planes, late_rows, 1)
 
-        first = (w_w, 0, E4M3)
-        second = (w2_w, 1, E5M2)
-        tokens = (xtg_w[:].bitcast(E2M1), tok_s)
-        notes = (xog_w[:].bitcast(E4M3), note_s)
+        matrix_w = (w_w, 0, E4M3)
+        matrix_w2 = (w2_w, 1, E5M2)
+        tokens = (xtg_w[:].bitcast(E2M1), planes[:, tok_cols])
+        notes = (xog_w[:].bitcast(E4M3), planes[:, note_cols])
 
-        def stage_one(acc, t, on_tokens, on_notes):
+        def first_stage(acc, t, on_tokens, on_notes):
             cols = slice(t * P, (t + 1) * P)
-            for (words, which, fmt), (rhs, rhs_scale), start in ((on_tokens, tokens, True), (on_notes, notes, False)):
-                at = 2 * J + t * pair + which * P
+            for (words, place, fmt), (rhs, rhs_scale), start in ((on_tokens, tokens, True), (on_notes, notes, False)):
+                at = (2 * t + place) * P
                 nc.tensor.matmul_mx(
                     out=acc, lhsT=words[:, cols].bitcast(fmt), lhsT_scale=planes[:, at : at + P],
                     rhs=rhs, rhs_scale=rhs_scale, start=start, stop=not start,
                 )
 
-        last = PACK - 1
         a_ps, b_ps = [], []
-        for t in range(last):
+        for t in range(PACK):
             b_ps.append(psum.tile([P, J], F32, name="b%d_ps" % t))
             a_ps.append(psum.tile([P, J], F32, name="a%d_ps" % t))
-            stage_one(b_ps[t][:], t, second, first)
-            stage_one(a_ps[t][:], t, first, second)
-        last_ps = psum.tile([P, 2 * J], F32, name="last_ps")
-        stage_one(last_ps[:, 0:J], last, first, second)
-        stage_one(last_ps[:, J:], last, second, first)
+            first_stage(b_ps[t][:], t, matrix_w2, matrix_w)
+            first_stage(a_ps[t][:], t, matrix_w, matrix_w2)
 
-        a_sb = [held("a%d" % t, [J], F32)[:] for t in range(last)]
-        b_sb = [held("b%d" % t, [J], F32)[:] for t in range(last)]
-        last_sb = held("last_sb", [2 * J], F32)
-        a_sb.append(last_sb[:, 0:J])
-        b_sb.append(last_sb[:, J:])
+        last = PACK - 1
+        half = O // HALVES
+        a_sb = [held("a%d" % t, [J], F32) for t in range(PACK)]
+        b_sb = [held("b%d" % t, [J], F32) for t in range(PACK)]
         pg = [held("pg%d" % t, [C], F32) for t in range(PACK)]
-        hid_rows = held("hid_rows", [PACK, O], BF16, tag="b1")
-        half = O // 2
+        hid_sets = held("hid_sets", [PACK, O], BF16)
 
-        for t in range(PACK):
-            for ahead in ((0,), (1, 2), (), ())[t]:
-                nc.scalar.copy(b_sb[ahead], b_ps[ahead][:])
-                nc.vector.tensor_copy(a_sb[ahead], a_ps[ahead][:])
-            if t + 1 == last:
-                nc.vector.tensor_copy(last_sb[:], last_ps[:])
-            nc.vector.tensor_copy(pw[t % 2][:].indirect(idx3[:]), a_sb[t])
-            nc.scalar.activation(pv[t % 2][:].indirect(idx4[:]), b_sb[t], COPY)
-            if t > 0:
-                nc.scalar.activation(hid_rows[:, t - 1, :], pg[t - 1][:].indirect(idx5[:]), COPY)
+        def empty(t):
+            nc.scalar.copy(b_sb[t][:], b_ps[t][:])
+            nc.vector.tensor_copy(a_sb[t][:], a_ps[t][:])
+
+        def put(t):
+            turn = t % HALVES
+            nc.vector.tensor_copy(pw[turn][:].indirect(idx3[:]), a_sb[t][:])
+            nc.scalar.activation(pv[turn][:].indirect(idx4[:]), b_sb[t][:], COPY)
             adder = nc.gpsimd if t < last else nc.vector
-            adder.tensor_tensor(pg[t][:], pw[t % 2][:], pv[t % 2][:], ADD)
-        nc.vector.tensor_copy(hid_rows[:, last, 0:half], pg[last][:].indirect(idx5[:, 0 : half // 16]))
-        nc.scalar.activation(hid_rows[:, last, half:O], pg[last][:].indirect(idx5[:, half // 16 : O // 16]), COPY)
+            adder.tensor_tensor(pg[t][:], pw[turn][:], pv[turn][:], ADD)
 
-        hid = [held("hid%d" % u, [half * PACK], BF16) for u in range(2)]
-        hid_w = [held("hid_w%d" % u, [half], U32) for u in range(2)]
-        hid_s = [held("hid_s%d" % u, [half], U8) for u in range(2)]
-        for u, weave in enumerate((nc.vector.tensor_copy, nc.scalar.copy)):
-            weave(
+        def read(t):
+            nc.scalar.activation(hid_sets[:, t, :], pg[t][:].indirect(idx5[:]), COPY)
+
+        empty(0)
+        put(0)
+        empty(1)
+        empty(2)
+        put(1)
+        empty(3)
+        read(0)
+        put(2)
+        put(3)
+        read(1)
+        read(2)
+        list_half = half // LIST_ROWS
+        nc.vector.tensor_copy(hid_sets[:, last, 0:half], pg[last][:].indirect(idx5[:, 0:list_half]))
+        nc.scalar.activation(hid_sets[:, last, half:O], pg[last][:].indirect(idx5[:, list_half : 2 * list_half]), COPY)
+
+        hid = [held("hid%d" % u, [half * PACK], BF16) for u in range(HALVES)]
+        hid_w = [held("hid_w%d" % u, [half], U32) for u in range(HALVES)]
+        hid_s = [held("hid_s%d" % u, [half], U8) for u in range(HALVES)]
+        for u in range(HALVES):
+            nc.vector.tensor_copy(
                 out=hid[u][:].rearrange("p (c i t) -> p c t i", t=PACK, i=4),
-                in_=hid_rows[:, :, u * half : (u + 1) * half].rearrange("p t (c i) -> p c t i", i=4),
+                in_=hid_sets[:, :, u * half : (u + 1) * half].rearrange("p t (c i) -> p c t i", i=4),
             )
+        for u in range(HALVES):
             nc.vector.quantize_mx(out=hid_w[u][:].bitcast(E5M2), scales=hid_s[u][:], in_=hid[u][:])
 
-        p_ps = []
-        for h, bank in enumerate(("b0_ps", "p1_ps")):
-            acc = psum.tile([P, O], F32, name="p%d_ps" % h, tag=bank)
-            cols = slice(h * P, (h + 1) * P)
-            nc.tensor.matmul_mx(
-                out=acc[:], lhsT=ws_w[:, cols].bitcast(E4M3), lhsT_scale=ws_s[:, cols],
-                rhs=sx_w.bitcast(E4M3), rhs_scale=sx_s, start=True, stop=False,
-            )
-            p_ps.append(acc)
-        for u in range(2):
-            for h in range(2):
+        p_sb = [held("p_sb%d" % h, [O], F32) for h in range(HALVES)]
+        left = [held("left%d" % h, [E], F32) for h in range(HALVES)]
+        right = [held("right%d" % h, [E], F32) for h in range(HALVES)]
+        best = [held("best%d" % h, [E], F32) for h in range(HALVES)]
+        p_ps = {}
+        for u in range(HALVES):
+            reads = slice(u * half, (u + 1) * half)
+            for h, bank in enumerate(("a%d_ps" % u, "b%d_ps" % u)):
+                p_ps[u, h] = psum.tile([P, half], F32, name="p%d%d_ps" % (u, h), tag=bank)
                 cols = slice(h * P, (h + 1) * P)
                 nc.tensor.matmul_mx(
-                    out=p_ps[h][:, u * half : (u + 1) * half],
-                    lhsT=wb_w.bitcast(E2M1)[:, cols], lhsT_scale=wb_s[:, cols],
-                    rhs=hid_w[u][:].bitcast(E5M2), rhs_scale=hid_s[u][:], start=False, stop=(u == 1),
+                    out=p_ps[u, h][:], lhsT=ws_w[:, cols].bitcast(E4M3), lhsT_scale=ws_s[:, cols],
+                    rhs=sx_w[:, reads].bitcast(E4M3), rhs_scale=sx_s[:, reads], start=True, stop=False,
                 )
+        for u in range(HALVES):
+            reads = slice(u * half, (u + 1) * half)
+            for h, move in enumerate((nc.vector.tensor_copy, nc.scalar.copy)):
+                cols = slice(h * P, (h + 1) * P)
+                nc.tensor.matmul_mx(
+                    out=p_ps[u, h][:], lhsT=wb_w.bitcast(E2M1)[:, cols], lhsT_scale=wb_s[:, cols],
+                    rhs=hid_w[u][:].bitcast(E5M2), rhs_scale=hid_s[u][:], start=False, stop=True,
+                )
+                move(p_sb[h][:, reads], p_ps[u, h][:])
 
-        p_sb = [held("p_sb%d" % h, [O], F32) for h in range(2)]
-        left = [held("left%d" % h, [E], F32) for h in range(2)]
-        right = [held("right%d" % h, [E], F32) for h in range(2)]
-        best = [held("best%d" % h, [E], F32) for h in range(2)]
-        nc.vector.tensor_copy(p_sb[0][:], p_ps[0][:])
-        nc.scalar.copy(p_sb[1][:], p_ps[1][:])
         nc.vector.tensor_copy(left[0][:], p_sb[0][:].indirect(idx6[:]))
         nc.vector.tensor_copy(right[0][:], p_sb[0][:].indirect(idx7[:]))
         nc.scalar.activation(left[1][:], p_sb[1][:].indirect(idx6[:]), COPY)
         nc.scalar.activation(right[1][:], p_sb[1][:].indirect(idx7[:]), COPY)
-        for h in range(2):
+        for h in range(HALVES):
             nc.vector.tensor_tensor(best[h][:], left[h][:], right[h][:], MAX)
             nc.sync.dma_start(out=out[h * P : (h + 1) * P, :], in_=best[h][:])

from contextlib import ExitStack

import concourse.mybir as mybir

K, T, Z, J, R, C, O, N, L, E = 512, 1024, 1024, 256, 512, 512, 256, 256, 512, 128
FLOPS = 4 * 2 * K * R * J + 2 * R * N * O + 2 * L * N * O

F32 = mybir.dt.float32
BF16 = mybir.dt.bfloat16
I32 = mybir.dt.int32
U32 = mybir.dt.uint32
U16 = mybir.dt.uint16
U8 = mybir.dt.uint8
E4M3 = mybir.dt.float8_e4m3fn_x4
E5M2 = mybir.dt.float8_e5m2_x4
E2M1 = mybir.dt.float4_e2m1fn_x4
COPY = mybir.ActivationFunctionType.Copy
ADD = mybir.AluOpType.add
MAX = mybir.AluOpType.max

P = 128
PACK = 4
QUAD = 32
QUADS = P // QUAD
QUAD_ROWS = 4
SCALE_ROWS = QUADS * QUAD_ROWS
TWICE = QUAD // SCALE_ROWS
LIST_ROWS = 16
LINE = 16
HALVES = 2


def load_scales_twice(queue, dst, scales):
    rows = scales[0].bitcast(I32)
    queue.dma_start(
        out=dst[0:QUAD, :].bitcast(I32),
        in_=rows.unsqueeze(1).broadcast_to([SCALE_ROWS, TWICE, rows.shape[1]]),
    )


def clear_upper_quadrants(engine, dst):
    engine.memset(dst[QUAD : 2 * QUAD, :].bitcast(I32), 0)
    engine.memset(dst[2 * QUAD : P, :].bitcast(I32), 0)


def load_scales(queue, dst, scales):
    queue.dma_start(out=dst[0:SCALE_ROWS, :].bitcast(I32), in_=scales[0].bitcast(I32))


def place_scales(queue, planes, staged, step):
    span = step * QUAD_ROWS
    for q in range(QUADS):
        queue.dma_start(
            out=planes[QUAD * q : QUAD * q + QUAD_ROWS, :].bitcast(I32),
            in_=staged[span * q : span * (q + 1) : step, :].bitcast(I32),
        )


def load_words8(queue, dst, words):
    queue.dma_start(out=dst.bitcast(I32), in_=words[0].rearrange("p c t -> p (c t)").bitcast(I32))


def load_words4(queue, dst, words):
    queue.dma_start(out=dst.bitcast(I32), in_=words[0].bitcast(I32))


def deal(move, dst, src, run):
    move(
        out=dst.rearrange("p (t c i) -> p c t i", t=PACK, i=run),
        in_=src.rearrange("p (c i t) -> p c t i", t=PACK, i=run),
    )


def tile_list_crossed_shared_skip_bestoftwo_kernel(
    tc, xt_words, xt_scales, xo_words, xo_scales, w_words, w_scales, w2_words, w2_scales,
    wb_words, wb_scales, sx_words, sx_scales, ws_words, ws_scales,
    offs, offs2, offs3, offs4, offs5, offs6, offs7, out,
):
    nc = tc.nc
    with ExitStack() as ctx:
        lists = ctx.enter_context(tc.tile_pool(name="lists", bufs=1))
        sb = ctx.enter_context(tc.tile_pool(name="sb", bufs=1))
        psum = ctx.enter_context(tc.psum_pool(name="psum", bufs=1))

        def list_tile(name, entries):
            return lists.tile([P, entries // LIST_ROWS], U16, name=name)

        def held(name, shape, dtype, tag=None):
            return sb.tile([P] + shape, dtype, name=name, tag=tag or name, align_bytes=64)

        idx, idx2 = list_tile("idx", J), list_tile("idx2", J)
        idx3, idx4, idx5 = list_tile("idx3", J), list_tile("idx4", J), list_tile("idx5", O)
        idx6, idx7 = list_tile("idx6", E), list_tile("idx7", E)

        xt_w, xt_s = held("xt_w", [T], U16), held("xt_s", [T], U8)
        xo_w, xo_s = held("xo_w", [Z], U32), held("xo_s", [Z], U8)
        w_raw, w2_raw = held("w_raw", [R], U32), held("w2_raw", [R], U32)
        raw_s = held("raw_s", [2 * R], U8)

        nc.sync.dma_start(idx[:], offs)
        load_scales_twice(nc.scalar, xo_s[:], xo_scales)
        nc.sync.dma_start(idx2[:], offs2)
        load_scales_twice(nc.scalar, xt_s[:], xt_scales)
        load_scales_twice(nc.sync, raw_s[:, 0:R], w_scales)
        load_scales_twice(nc.scalar, raw_s[:, R : 2 * R], w2_scales)
        load_words8(nc.sync, xo_w[:], xo_words)
        load_words4(nc.scalar, xt_w[:], xt_words)
        nc.sync.dma_start(idx3[:], offs3)
        nc.sync.dma_start(idx4[:], offs4)
        nc.sync.dma_start(idx5[:], offs5)
        load_words8(nc.sync, w_raw[:], w_words)
        load_words8(nc.sync, w2_raw[:], w2_words)

        first_width = 2 * R + 2 * J
        tok_cols, note_cols = slice(2 * R, 2 * R + J), slice(2 * R + J, first_width)
        rows = held("rows", [first_width], U8)
        planes = held("planes", [first_width], U8)
        for staged in (xt_s, xo_s, raw_s):
            clear_upper_quadrants(nc.vector, staged)
        nc.gpsimd.memset(planes[:].bitcast(I32), 0)

        w_w, w2_w = held("w_w", [R], U32), held("w2_w", [R], U32)
        xtg_w, xtg_s = held("xtg_w", [J], U16), held("xtg_s", [J], U8)
        xog_w, xog_s = held("xog_w", [J], U32), held("xog_s", [J], U8)

        nc.vector.tensor_copy(xtg_s[:], xt_s[:].indirect(idx[:]))
        nc.vector.tensor_copy(xog_s[:], xo_s[:].indirect(idx2[:]))
        deal(nc.gpsimd.tensor_copy, rows[:, 0 : 2 * R], raw_s[:], LINE)
        nc.vector.tensor_copy(rows[:, tok_cols].bitcast(I32), xtg_s[:].bitcast(I32))
        nc.vector.tensor_copy(rows[:, note_cols].bitcast(I32), xog_s[:].bitcast(I32))
        place_scales(nc.sync, planes, rows, TWICE)
        nc.sync.dma_start(idx6[:], offs6)
        nc.sync.dma_start(idx7[:], offs7)
        nc.vector.tensor_copy(xog_w[:], xo_w[:].indirect(idx2[:]))
        nc.vector.tensor_copy(xtg_w[:], xt_w[:].indirect(idx[:]))
        deal(nc.scalar.copy, w_w[:], w_raw[:], LINE // 4)
        deal(nc.scalar.copy, w2_w[:], w2_raw[:], LINE // 4)

        pw = [held("pw0", [C], F32, tag="xo_w"), held("pw1", [C], F32, tag="w2_raw")]
        pv = [held("pv0", [C], F32, tag="xt_w"), held("pv1", [C], F32, tag="w_raw")]
        for turn, engine in enumerate((nc.vector, nc.gpsimd)):
            engine.memset(pv[turn][:], 0.0)
            engine.memset(pw[turn][:], 0.0)

        second_width = N + O + N
        late_rows = held("late_rows", [second_width], U8, tag="raw_s")
        late_planes = held("late_planes", [second_width], U8)
        wb_s, sx_s, ws_s = late_planes[:, 0:N], late_planes[:, N : N + O], late_planes[:, N + O :]
        late_w = held("late_w", [N + O + N // 2], U32, tag="rows")
        ws_w, sx_w, wb_w = late_w[:, 0:N], late_w[:, N : N + O], late_w[:, N + O :]
        nc.gpsimd.memset(late_planes[:].bitcast(I32), 0)
        load_scales(nc.sync, late_rows[:, 0:N], wb_scales)
        load_scales(nc.sync, late_rows[:, N : N + O], sx_scales)
        load_scales(nc.sync, late_rows[:, N + O :], ws_scales)
        load_words8(nc.sync, ws_w, ws_words)
        load_words8(nc.sync, sx_w, sx_words)
        load_words4(nc.sync, wb_w, wb_words)
        place_scales(nc.sync, late_planes, late_rows, 1)

        matrix_w = (w_w, 0, E4M3)
        matrix_w2 = (w2_w, 1, E5M2)
        tokens = (xtg_w[:].bitcast(E2M1), planes[:, tok_cols])
        notes = (xog_w[:].bitcast(E4M3), planes[:, note_cols])

        def first_stage(acc, t, on_tokens, on_notes):
            cols = slice(t * P, (t + 1) * P)
            for (words, place, fmt), (rhs, rhs_scale), start in ((on_tokens, tokens, True), (on_notes, notes, False)):
                at = (2 * t + place) * P
                nc.tensor.matmul_mx(
                    out=acc, lhsT=words[:, cols].bitcast(fmt), lhsT_scale=planes[:, at : at + P],
                    rhs=rhs, rhs_scale=rhs_scale, start=start, stop=not start,
                )

        a_ps, b_ps = [], []
        for t in range(PACK):
            b_ps.append(psum.tile([P, J], F32, name="b%d_ps" % t))
            a_ps.append(psum.tile([P, J], F32, name="a%d_ps" % t))
            first_stage(b_ps[t][:], t, matrix_w2, matrix_w)
            first_stage(a_ps[t][:], t, matrix_w, matrix_w2)

        last = PACK - 1
        half = O // HALVES
        a_sb = [held("a%d" % t, [J], F32) for t in range(PACK)]
        b_sb = [held("b%d" % t, [J], F32) for t in range(PACK)]
        pg = [held("pg%d" % t, [C], F32) for t in range(PACK)]
        hid_sets = held("hid_sets", [PACK, O], BF16)

        def empty(t):
            nc.scalar.copy(b_sb[t][:], b_ps[t][:])
            nc.vector.tensor_copy(a_sb[t][:], a_ps[t][:])

        def put(t):
            turn = t % HALVES
            nc.vector.tensor_copy(pw[turn][:].indirect(idx3[:]), a_sb[t][:])
            nc.scalar.activation(pv[turn][:].indirect(idx4[:]), b_sb[t][:], COPY)
            adder = nc.gpsimd if t < last else nc.vector
            adder.tensor_tensor(pg[t][:], pw[turn][:], pv[turn][:], ADD)

        def read(t):
            nc.scalar.activation(hid_sets[:, t, :], pg[t][:].indirect(idx5[:]), COPY)

        empty(0)
        put(0)
        empty(1)
        empty(2)
        put(1)
        empty(3)
        read(0)
        put(2)
        put(3)
        read(1)
        read(2)
        list_half = half // LIST_ROWS
        nc.vector.tensor_copy(hid_sets[:, last, 0:half], pg[last][:].indirect(idx5[:, 0:list_half]))
        nc.scalar.activation(hid_sets[:, last, half:O], pg[last][:].indirect(idx5[:, list_half : 2 * list_half]), COPY)

        hid = [held("hid%d" % u, [half * PACK], BF16) for u in range(HALVES)]
        hid_w = [held("hid_w%d" % u, [half], U32) for u in range(HALVES)]
        hid_s = [held("hid_s%d" % u, [half], U8) for u in range(HALVES)]
        for u in range(HALVES):
            nc.vector.tensor_copy(
                out=hid[u][:].rearrange("p (c i t) -> p c t i", t=PACK, i=4),
                in_=hid_sets[:, :, u * half : (u + 1) * half].rearrange("p t (c i) -> p c t i", i=4),
            )
        for u in range(HALVES):
            nc.vector.quantize_mx(out=hid_w[u][:].bitcast(E5M2), scales=hid_s[u][:], in_=hid[u][:])

        p_sb = [held("p_sb%d" % h, [O], F32) for h in range(HALVES)]
        left = [held("left%d" % h, [E], F32) for h in range(HALVES)]
        right = [held("right%d" % h, [E], F32) for h in range(HALVES)]
        best = [held("best%d" % h, [E], F32) for h in range(HALVES)]
        p_ps = {}
        for u in range(HALVES):
            reads = slice(u * half, (u + 1) * half)
            for h, bank in enumerate(("a%d_ps" % u, "b%d_ps" % u)):
                p_ps[u, h] = psum.tile([P, half], F32, name="p%d%d_ps" % (u, h), tag=bank)
                cols = slice(h * P, (h + 1) * P)
                nc.tensor.matmul_mx(
                    out=p_ps[u, h][:], lhsT=ws_w[:, cols].bitcast(E4M3), lhsT_scale=ws_s[:, cols],
                    rhs=sx_w[:, reads].bitcast(E4M3), rhs_scale=sx_s[:, reads], start=True, stop=False,
                )
        for u in range(HALVES):
            reads = slice(u * half, (u + 1) * half)
            for h, move in enumerate((nc.vector.tensor_copy, nc.scalar.copy)):
                cols = slice(h * P, (h + 1) * P)
                nc.tensor.matmul_mx(
                    out=p_ps[u, h][:], lhsT=wb_w.bitcast(E2M1)[:, cols], lhsT_scale=wb_s[:, cols],
                    rhs=hid_w[u][:].bitcast(E5M2), rhs_scale=hid_s[u][:], start=False, stop=True,
                )
                move(p_sb[h][:, reads], p_ps[u, h][:])

        nc.vector.tensor_copy(left[0][:], p_sb[0][:].indirect(idx6[:]))
        nc.vector.tensor_copy(right[0][:], p_sb[0][:].indirect(idx7[:]))
        nc.scalar.activation(left[1][:], p_sb[1][:].indirect(idx6[:]), COPY)
        nc.scalar.activation(right[1][:], p_sb[1][:].indirect(idx7[:]), COPY)
        for h in range(HALVES):
            nc.vector.tensor_tensor(best[h][:], left[h][:], right[h][:], MAX)
            nc.sync.dma_start(out=out[h * P : (h + 1) * P, :], in_=best[h][:])
